import numpy as np
import ml_dtypes

BF16 = ml_dtypes.bfloat16


def bf(x):
    return np.asarray(x, np.float32).astype(BF16)


def f32(x):
    return np.asarray(x, np.float32)


def f64(x):
    return np.asarray(x).astype(np.float64)


def striped(idx):
    return np.tile(idx.reshape(-1, 16).T, (8, 1))


S, K, M, N, D, V = 2048, 512, 256, 1024, 2, 512


def sigmoid(v):
    return 1.0 / (1.0 + np.exp(-v))


def setup_inputs():
    return {"table": bf(np.random.standard_normal((K, S))), "w": bf(np.random.standard_normal((D, K, M)) / np.sqrt(D * K)), "b": f32(0.5 * np.random.standard_normal((M, 1))), "offs": striped(np.random.permutation(S)[:N])}


def reference(table, w, b, offs):
    idx = offs[:16].T.reshape(-1)
    x = f64(table)[:, idx]
    y = sum(f64(w)[t].T @ x[:, t * V : (t + 1) * V] for t in range(D))
    return (y + f64(b)) * sigmoid(y + f64(b))

@@ -1,0 +1,60 @@
+import concourse.mybir as mybir
+
+BF16 = mybir.dt.bfloat16
+F32 = mybir.dt.float32
+U16 = mybir.dt.uint16
+SILU = mybir.ActivationFunctionType.Silu
+
+P = 128
+K, S = 512, 2048
+ENDS, M, V = 2, 256, 512
+K_BLOCKS = K // P
+M_BLOCKS = M // P
+LIST_COLUMNS = V // 16
+
+FLOPS = 2 * ENDS * K * M * V
+
+
+def tile_gather_matmul_kernel(tc, table, w, b, offs, out):
+    nc = tc.nc
+    with (
+        tc.tile_pool(name="held", bufs=1) as held,
+        tc.psum_pool(name="psum", bufs=1) as psum,
+    ):
+        offsets = held.tile([P, ENDS * LIST_COLUMNS], U16, name="offsets")
+        nc.sync.dma_start(offsets[:], offs)
+
+        table_blocks = []
+        weight_blocks = []
+        for kb in range(K_BLOCKS):
+            rows = slice(kb * P, (kb + 1) * P)
+            table_block = held.tile([P, S], BF16, name="table%d" % kb)
+            nc.sync.dma_start(table_block[:], table[rows, :])
+            table_blocks.append(table_block)
+            weight_block = held.tile([P, ENDS, M], BF16, name="weights%d" % kb)
+            nc.scalar.dma_start(weight_block[:], w[:, rows, :].rearrange("t p m -> p t m"))
+            weight_blocks.append(weight_block)
+
+        bias = held.tile([P, M_BLOCKS], F32, name="bias")
+        with nc.allow_non_contiguous_dma(reason="256 single float32 values, one to a partition and block"):
+            nc.scalar.dma_start(bias[:], b.rearrange("(a p) o -> p (a o)", p=P))
+
+        banks = [psum.tile([P, V], F32, name="bank%d" % mb) for mb in range(M_BLOCKS)]
+        for kb in range(K_BLOCKS):
+            for mb in range(M_BLOCKS):
+                for end in range(ENDS):
+                    picked = table_blocks[kb][:].indirect(
+                        offsets[:, end * LIST_COLUMNS : (end + 1) * LIST_COLUMNS]
+                    )
+                    nc.tensor.matmul(
+                        banks[mb][:],
+                        weight_blocks[kb][:, end, mb * P : (mb + 1) * P],
+                        picked,
+                        start=(kb == 0 and end == 0),
+                        stop=(kb == K_BLOCKS - 1 and end == ENDS - 1),
+                    )
+
+        for mb in range(M_BLOCKS):
+            result = held.tile([P, V], F32, name="result%d" % mb)
+            nc.scalar.activation(result[:], banks[mb][:], SILU, bias=bias[:, mb : mb + 1])
+            nc.sync.dma_start(out[mb * P : (mb + 1) * P, :], result[:])

@@ -28,12 +28,13 @@ def tile_gather_matmul_kernel(tc, table, w, b, offs, out):
         weight_blocks = []
         for kb in range(K_BLOCKS):
             rows = slice(kb * P, (kb + 1) * P)
+            weight_block = held.tile([P, ENDS, M], BF16, name="weights%d" % kb)
+            weight_queue = nc.scalar if kb == 0 else nc.sync
+            weight_queue.dma_start(weight_block[:], w[:, rows, :].rearrange("t p m -> p t m"))
+            weight_blocks.append(weight_block)
             table_block = held.tile([P, S], BF16, name="table%d" % kb)
             nc.sync.dma_start(table_block[:], table[rows, :])
             table_blocks.append(table_block)
-            weight_block = held.tile([P, ENDS, M], BF16, name="weights%d" % kb)
-            nc.scalar.dma_start(weight_block[:], w[:, rows, :].rearrange("t p m -> p t m"))
-            weight_blocks.append(weight_block)
 
         bias = held.tile([P, M_BLOCKS], F32, name="bias")
         with nc.allow_non_contiguous_dma(reason="256 single float32 values, one to a partition and block"):

@@ -11,6 +11,7 @@ ENDS, M, V = 2, 256, 512
 K_BLOCKS = K // P
 M_BLOCKS = M // P
 LIST_COLUMNS = V // 16
+WARM_MATMULS = 5
 
 FLOPS = 2 * ENDS * K * M * V
 
@@ -39,6 +40,12 @@ def tile_gather_matmul_kernel(tc, table, w, b, offs, out):
         bias = held.tile([P, M_BLOCKS], F32, name="bias")
         with nc.allow_non_contiguous_dma(reason="256 single float32 values, one to a partition and block"):
             nc.scalar.dma_start(bias[:], b.rearrange("(a p) o -> p (a o)", p=P))
+
+        zeros = held.tile([P, V], BF16, name="zeros")
+        nc.vector.memset(zeros[:], 0.0)
+        unread = psum.tile([P, V], F32, name="unread")
+        for repeat in range(WARM_MATMULS):
+            nc.tensor.matmul(unread[:], zeros[:, 0:P], zeros[:], start=True, stop=True)
 
         banks = [psum.tile([P, V], F32, name="bank%d" % mb) for mb in range(M_BLOCKS)]
         for kb in range(K_BLOCKS):

@@ -10,8 +10,8 @@ K, S = 512, 2048
 ENDS, M, V = 2, 256, 512
 K_BLOCKS = K // P
 M_BLOCKS = M // P
+HALF = V // 2
 LIST_COLUMNS = V // 16
-WARM_MATMULS = 5
 
 FLOPS = 2 * ENDS * K * M * V
 
@@ -41,12 +41,6 @@ def tile_gather_matmul_kernel(tc, table, w, b, offs, out):
         with nc.allow_non_contiguous_dma(reason="256 single float32 values, one to a partition and block"):
             nc.scalar.dma_start(bias[:], b.rearrange("(a p) o -> p (a o)", p=P))
 
-        zeros = held.tile([P, V], BF16, name="zeros")
-        nc.vector.memset(zeros[:], 0.0)
-        unread = psum.tile([P, V], F32, name="unread")
-        for repeat in range(WARM_MATMULS):
-            nc.tensor.matmul(unread[:], zeros[:, 0:P], zeros[:], start=True, stop=True)
-
         banks = [psum.tile([P, V], F32, name="bank%d" % mb) for mb in range(M_BLOCKS)]
         for kb in range(K_BLOCKS):
             for mb in range(M_BLOCKS):
@@ -63,6 +57,8 @@ def tile_gather_matmul_kernel(tc, table, w, b, offs, out):
                     )
 
         for mb in range(M_BLOCKS):
-            result = held.tile([P, V], F32, name="result%d" % mb)
-            nc.scalar.activation(result[:], banks[mb][:], SILU, bias=bias[:, mb : mb + 1])
-            nc.sync.dma_start(out[mb * P : (mb + 1) * P, :], result[:])
+            for half in range(2):
+                columns = slice(half * HALF, (half + 1) * HALF)
+                result = held.tile([P, HALF], F32, name="result%d_%d" % (mb, half))
+                nc.scalar.activation(result[:], banks[mb][:, columns], SILU, bias=bias[:, mb : mb + 1])
+                nc.sync.dma_start(out[mb * P : (mb + 1) * P, columns], result[:])

@@ -30,11 +30,11 @@ def tile_gather_matmul_kernel(tc, table, w, b, offs, out):
         for kb in range(K_BLOCKS):
             rows = slice(kb * P, (kb + 1) * P)
             weight_block = held.tile([P, ENDS, M], BF16, name="weights%d" % kb)
-            weight_queue = nc.scalar if kb == 0 else nc.sync
+            weight_queue = nc.sync if kb == 0 else nc.scalar
             weight_queue.dma_start(weight_block[:], w[:, rows, :].rearrange("t p m -> p t m"))
             weight_blocks.append(weight_block)
             table_block = held.tile([P, S], BF16, name="table%d" % kb)
-            nc.sync.dma_start(table_block[:], table[rows, :])
+            nc.scalar.dma_start(table_block[:], table[rows, :])
             table_blocks.append(table_block)
 
         bias = held.tile([P, M_BLOCKS], F32, name="bias")

@@ -25,17 +25,24 @@ def tile_gather_matmul_kernel(tc, table, w, b, offs, out):
         offsets = held.tile([P, ENDS * LIST_COLUMNS], U16, name="offsets")
         nc.sync.dma_start(offsets[:], offs)
 
-        table_blocks = []
-        weight_blocks = []
+        table_blocks = [held.tile([P, S], BF16, name="table%d" % kb) for kb in range(K_BLOCKS)]
+
+        w_matrices = w.rearrange("t (kb p) m -> p (t kb) m", p=P)
+
+        weights_of = {}
+        first_weights = held.tile([P, M], BF16, name="first_weights")
+        nc.sync.dma_start(first_weights[:], w_matrices[:, 0, :])
+        weights_of[(0, 0)] = first_weights[:]
         for kb in range(K_BLOCKS):
-            rows = slice(kb * P, (kb + 1) * P)
-            weight_block = held.tile([P, ENDS, M], BF16, name="weights%d" % kb)
-            weight_queue = nc.sync if kb == 0 else nc.scalar
-            weight_queue.dma_start(weight_block[:], w[:, rows, :].rearrange("t p m -> p t m"))
-            weight_blocks.append(weight_block)
-            table_block = held.tile([P, S], BF16, name="table%d" % kb)
-            nc.scalar.dma_start(table_block[:], table[rows, :])
-            table_blocks.append(table_block)
+            nc.scalar.dma_start(table_blocks[kb][:], table[kb * P : (kb + 1) * P, :])
+            if kb < K_BLOCKS - 1:
+                between = held.tile([P, 2, M], BF16, name="weights_between%d" % kb)
+                nc.scalar.dma_start(between[:], w_matrices[:, kb + 1 : kb + 1 + K_BLOCKS : K_BLOCKS - 1, :])
+                weights_of[(kb + 1, 0)] = between[:, 0, :]
+                weights_of[(kb, 1)] = between[:, 1, :]
+        last_weights = held.tile([P, M], BF16, name="last_weights")
+        nc.scalar.dma_start(last_weights[:], w_matrices[:, ENDS * K_BLOCKS - 1, :])
+        weights_of[(K_BLOCKS - 1, 1)] = last_weights[:]
 
         bias = held.tile([P, M_BLOCKS], F32, name="bias")
         with nc.allow_non_contiguous_dma(reason="256 single float32 values, one to a partition and block"):
@@ -50,7 +57,7 @@ def tile_gather_matmul_kernel(tc, table, w, b, offs, out):
                     )
                     nc.tensor.matmul(
                         banks[mb][:],
-                        weight_blocks[kb][:, end, mb * P : (mb + 1) * P],
+                        weights_of[(kb, end)][:, mb * P : (mb + 1) * P],
                         picked,
                         start=(kb == 0 and end == 0),
                         stop=(kb == K_BLOCKS - 1 and end == ENDS - 1),

@@ -11,9 +11,15 @@ ENDS, M, V = 2, 256, 512
 K_BLOCKS = K // P
 M_BLOCKS = M // P
 HALF = V // 2
+LATE = 2
 LIST_COLUMNS = V // 16
 
 FLOPS = 2 * ENDS * K * M * V
+
+
+def keep(weights_of, kb, end, matrix):
+    for mb in range(M_BLOCKS):
+        weights_of[(kb, end, mb)] = matrix[:, mb * P : (mb + 1) * P]
 
 
 def tile_gather_matmul_kernel(tc, table, w, b, offs, out):
@@ -32,36 +38,46 @@ def tile_gather_matmul_kernel(tc, table, w, b, offs, out):
         weights_of = {}
         first_weights = held.tile([P, M], BF16, name="first_weights")
         nc.sync.dma_start(first_weights[:], w_matrices[:, 0, :])
-        weights_of[(0, 0)] = first_weights[:]
-        for kb in range(K_BLOCKS):
-            nc.scalar.dma_start(table_blocks[kb][:], table[kb * P : (kb + 1) * P, :])
-            if kb < K_BLOCKS - 1:
-                between = held.tile([P, 2, M], BF16, name="weights_between%d" % kb)
-                nc.scalar.dma_start(between[:], w_matrices[:, kb + 1 : kb + 1 + K_BLOCKS : K_BLOCKS - 1, :])
-                weights_of[(kb + 1, 0)] = between[:, 0, :]
-                weights_of[(kb, 1)] = between[:, 1, :]
-        last_weights = held.tile([P, M], BF16, name="last_weights")
-        nc.scalar.dma_start(last_weights[:], w_matrices[:, ENDS * K_BLOCKS - 1, :])
-        weights_of[(K_BLOCKS - 1, 1)] = last_weights[:]
+        keep(weights_of, 0, 0, first_weights[:])
+        nc.scalar.dma_start(table_blocks[0][:], table[0:P, :])
+        between = held.tile([P, 2, M], BF16, name="between")
+        nc.scalar.dma_start(between[:], w_matrices[:, 1 : 1 + K_BLOCKS : K_BLOCKS - 1, :])
+        keep(weights_of, 1, 0, between[:, 0, :])
+        keep(weights_of, 0, 1, between[:, 1, :])
+        nc.scalar.dma_start(table_blocks[1][:], table[P : 2 * P, :])
+        block1_targets = held.tile([P, M], BF16, name="block1_targets")
+        nc.scalar.dma_start(block1_targets[:], w_matrices[:, K_BLOCKS + 1, :])
+        keep(weights_of, 1, 1, block1_targets[:])
+        late_early = held.tile([P, ENDS, P], BF16, name="late_early")
+        nc.scalar.dma_start(late_early[:], w_matrices[:, LATE::K_BLOCKS, 0:P])
+        nc.scalar.dma_start(table_blocks[2][:], table[2 * P : 3 * P, :])
+        block3_weights = held.tile([P, ENDS, M], BF16, name="block3_weights")
+        nc.scalar.dma_start(block3_weights[:], w_matrices[:, 3::K_BLOCKS, :])
+        nc.scalar.dma_start(table_blocks[3][:], table[3 * P : 4 * P, :])
+        late_late = held.tile([P, ENDS, P], BF16, name="late_late")
+        nc.scalar.dma_start(late_late[:], w_matrices[:, LATE::K_BLOCKS, P : 2 * P])
+        for end in range(ENDS):
+            keep(weights_of, 3, end, block3_weights[:, end, :])
+            weights_of[(LATE, end, 0)] = late_early[:, end, :]
+            weights_of[(LATE, end, 1)] = late_late[:, end, :]
 
         bias = held.tile([P, M_BLOCKS], F32, name="bias")
         with nc.allow_non_contiguous_dma(reason="256 single float32 values, one to a partition and block"):
             nc.scalar.dma_start(bias[:], b.rearrange("(a p) o -> p (a o)", p=P))
 
         banks = [psum.tile([P, V], F32, name="bank%d" % mb) for mb in range(M_BLOCKS)]
-        for kb in range(K_BLOCKS):
-            for mb in range(M_BLOCKS):
-                for end in range(ENDS):
-                    picked = table_blocks[kb][:].indirect(
-                        offsets[:, end * LIST_COLUMNS : (end + 1) * LIST_COLUMNS]
-                    )
-                    nc.tensor.matmul(
-                        banks[mb][:],
-                        weights_of[(kb, end)][:, mb * P : (mb + 1) * P],
-                        picked,
-                        start=(kb == 0 and end == 0),
-                        stop=(kb == K_BLOCKS - 1 and end == ENDS - 1),
-                    )
+        order = [(kb, mb) for kb in range(K_BLOCKS) for mb in range(M_BLOCKS) if (kb, mb) != (LATE, 1)]
+        order.append((LATE, 1))
+        for kb, mb in order:
+            last_of_bank = LATE if mb == 1 else K_BLOCKS - 1
+            for end in range(ENDS):
+                nc.tensor.matmul(
+                    banks[mb][:],
+                    weights_of[(kb, end, mb)],
+                    table_blocks[kb][:].indirect(offsets[:, end * LIST_COLUMNS : (end + 1) * LIST_COLUMNS]),
+                    start=(kb == 0 and end == 0),
+                    stop=(kb == last_of_bank and end == ENDS - 1),
+                )
 
         for mb in range(M_BLOCKS):
             for half in range(2):

@@ -11,15 +11,10 @@ ENDS, M, V = 2, 256, 512
 K_BLOCKS = K // P
 M_BLOCKS = M // P
 HALF = V // 2
-LATE = 2
+LATE = K_BLOCKS - 1
 LIST_COLUMNS = V // 16
 
 FLOPS = 2 * ENDS * K * M * V
-
-
-def keep(weights_of, kb, end, matrix):
-    for mb in range(M_BLOCKS):
-        weights_of[(kb, end, mb)] = matrix[:, mb * P : (mb + 1) * P]
 
 
 def tile_gather_matmul_kernel(tc, table, w, b, offs, out):
@@ -31,52 +26,53 @@ def tile_gather_matmul_kernel(tc, table, w, b, offs, out):
         offsets = held.tile([P, ENDS * LIST_COLUMNS], U16, name="offsets")
         nc.sync.dma_start(offsets[:], offs)
 
+        table_dealt = table.rearrange("(p kb) s -> p kb s", kb=K_BLOCKS)
+        w_dealt = w.rearrange("t (p kb) m -> p t (kb m)", kb=K_BLOCKS)
         table_blocks = [held.tile([P, S], BF16, name="table%d" % kb) for kb in range(K_BLOCKS)]
-
-        w_matrices = w.rearrange("t (kb p) m -> p (t kb) m", p=P)
-
         weights_of = {}
+
+        early = K_BLOCKS * M - P
         first_weights = held.tile([P, M], BF16, name="first_weights")
-        nc.sync.dma_start(first_weights[:], w_matrices[:, 0, :])
-        keep(weights_of, 0, 0, first_weights[:])
-        nc.scalar.dma_start(table_blocks[0][:], table[0:P, :])
-        between = held.tile([P, 2, M], BF16, name="between")
-        nc.scalar.dma_start(between[:], w_matrices[:, 1 : 1 + K_BLOCKS : K_BLOCKS - 1, :])
-        keep(weights_of, 1, 0, between[:, 0, :])
-        keep(weights_of, 0, 1, between[:, 1, :])
-        nc.scalar.dma_start(table_blocks[1][:], table[P : 2 * P, :])
-        block1_targets = held.tile([P, M], BF16, name="block1_targets")
-        nc.scalar.dma_start(block1_targets[:], w_matrices[:, K_BLOCKS + 1, :])
-        keep(weights_of, 1, 1, block1_targets[:])
-        late_early = held.tile([P, ENDS, P], BF16, name="late_early")
-        nc.scalar.dma_start(late_early[:], w_matrices[:, LATE::K_BLOCKS, 0:P])
-        nc.scalar.dma_start(table_blocks[2][:], table[2 * P : 3 * P, :])
-        block3_weights = held.tile([P, ENDS, M], BF16, name="block3_weights")
-        nc.scalar.dma_start(block3_weights[:], w_matrices[:, 3::K_BLOCKS, :])
-        nc.scalar.dma_start(table_blocks[3][:], table[3 * P : 4 * P, :])
-        late_late = held.tile([P, ENDS, P], BF16, name="late_late")
-        nc.scalar.dma_start(late_late[:], w_matrices[:, LATE::K_BLOCKS, P : 2 * P])
-        for end in range(ENDS):
-            keep(weights_of, 3, end, block3_weights[:, end, :])
-            weights_of[(LATE, end, 0)] = late_early[:, end, :]
-            weights_of[(LATE, end, 1)] = late_late[:, end, :]
+        nc.sync.dma_start(first_weights[:], w_dealt[:, 0, 0:M])
+        nc.scalar.dma_start(table_blocks[0][:], table_dealt[:, 0, :])
+        targets_weights = held.tile([P, early], BF16, name="targets_weights")
+        nc.scalar.dma_start(targets_weights[:], w_dealt[:, 1, 0:early])
+        nc.scalar.dma_start(table_blocks[1][:], table_dealt[:, 1, :])
+        sources_weights = held.tile([P, early - M], BF16, name="sources_weights")
+        nc.scalar.dma_start(sources_weights[:], w_dealt[:, 0, M:early])
+        nc.scalar.dma_start(table_blocks[LATE][:], table_dealt[:, LATE, :])
+        nc.scalar.dma_start(table_blocks[2][:], table_dealt[:, 2, :])
+        late_weights = held.tile([P, ENDS, P], BF16, name="late_weights")
+        nc.scalar.dma_start(late_weights[:], w_dealt[:, :, early : early + P])
+        for kb in range(K_BLOCKS):
+            for mb in range(M_BLOCKS):
+                column = kb * M + mb * P
+                if column == early:
+                    weights_of[(kb, 0, mb)] = late_weights[:, 0, :]
+                    weights_of[(kb, 1, mb)] = late_weights[:, 1, :]
+                else:
+                    weights_of[(kb, 1, mb)] = targets_weights[:, column : column + P]
+                    weights_of[(kb, 0, mb)] = (
+                        first_weights[:, column : column + P]
+                        if kb == 0
+                        else sources_weights[:, column - M : column - M + P]
+                    )
 
         bias = held.tile([P, M_BLOCKS], F32, name="bias")
         with nc.allow_non_contiguous_dma(reason="256 single float32 values, one to a partition and block"):
             nc.scalar.dma_start(bias[:], b.rearrange("(a p) o -> p (a o)", p=P))
 
         banks = [psum.tile([P, V], F32, name="bank%d" % mb) for mb in range(M_BLOCKS)]
-        order = [(kb, mb) for kb in range(K_BLOCKS) for mb in range(M_BLOCKS) if (kb, mb) != (LATE, 1)]
-        order.append((LATE, 1))
+        order = [(0, 0), (0, 1), (1, 0), (1, 1), (LATE, 0), (2, 0), (2, 1), (LATE, 1)]
         for kb, mb in order:
-            last_of_bank = LATE if mb == 1 else K_BLOCKS - 1
-            for end in range(ENDS):
+            ends = (0, 1) if kb == 0 else (1, 0)
+            for end in ends:
                 nc.tensor.matmul(
                     banks[mb][:],
                     weights_of[(kb, end, mb)],
                     table_blocks[kb][:].indirect(offsets[:, end * LIST_COLUMNS : (end + 1) * LIST_COLUMNS]),
-                    start=(kb == 0 and end == 0),
-                    stop=(kb == last_of_bank and end == ENDS - 1),
+                    start=(kb == 0 and end == ends[0]),
+                    stop=(kb == (LATE if mb == 1 else 2) and end == ends[1]),
                 )
 
         for mb in range(M_BLOCKS):

@@ -31,32 +31,28 @@ def tile_gather_matmul_kernel(tc, table, w, b, offs, out):
         table_blocks = [held.tile([P, S], BF16, name="table%d" % kb) for kb in range(K_BLOCKS)]
         weights_of = {}
 
-        early = K_BLOCKS * M - P
-        first_weights = held.tile([P, M], BF16, name="first_weights")
-        nc.sync.dma_start(first_weights[:], w_dealt[:, 0, 0:M])
-        nc.scalar.dma_start(table_blocks[0][:], table_dealt[:, 0, :])
-        targets_weights = held.tile([P, early], BF16, name="targets_weights")
-        nc.scalar.dma_start(targets_weights[:], w_dealt[:, 1, 0:early])
-        nc.scalar.dma_start(table_blocks[1][:], table_dealt[:, 1, :])
-        sources_weights = held.tile([P, early - M], BF16, name="sources_weights")
-        nc.scalar.dma_start(sources_weights[:], w_dealt[:, 0, M:early])
-        nc.scalar.dma_start(table_blocks[LATE][:], table_dealt[:, LATE, :])
-        nc.scalar.dma_start(table_blocks[2][:], table_dealt[:, 2, :])
-        late_weights = held.tile([P, ENDS, P], BF16, name="late_weights")
-        nc.scalar.dma_start(late_weights[:], w_dealt[:, :, early : early + P])
-        for kb in range(K_BLOCKS):
-            for mb in range(M_BLOCKS):
-                column = kb * M + mb * P
-                if column == early:
-                    weights_of[(kb, 0, mb)] = late_weights[:, 0, :]
-                    weights_of[(kb, 1, mb)] = late_weights[:, 1, :]
-                else:
-                    weights_of[(kb, 1, mb)] = targets_weights[:, column : column + P]
-                    weights_of[(kb, 0, mb)] = (
-                        first_weights[:, column : column + P]
-                        if kb == 0
-                        else sources_weights[:, column - M : column - M + P]
-                    )
+        def load_weights(queue, ends, first, last):
+            piece = held.tile([P, ends.stop - ends.start, last - first], BF16, name="weights%d_%d" % (ends.start, first))
+            queue.dma_start(piece[:], w_dealt[:, ends, first:last])
+            for end in range(ends.start, ends.stop):
+                for column in range(first, last, P):
+                    weights_of[(end, column)] = piece[:, end - ends.start, column - first : column - first + P]
+
+        def load_table(kb):
+            nc.scalar.dma_start(table_blocks[kb][:], table_dealt[:, kb, :])
+
+        sources, targets, both = slice(0, 1), slice(1, 2), slice(0, 2)
+        late_column = LATE * M + P
+        load_weights(nc.sync, sources, 0, P)
+        load_table(0)
+        load_weights(nc.scalar, sources, P, M)
+        load_weights(nc.scalar, targets, 0, M)
+        load_table(1)
+        load_weights(nc.scalar, sources, M, late_column)
+        load_weights(nc.scalar, targets, M, late_column)
+        load_table(LATE)
+        load_table(2)
+        load_weights(nc.scalar, both, late_column, late_column + P)
 
         bias = held.tile([P, M_BLOCKS], F32, name="bias")
         with nc.allow_non_contiguous_dma(reason="256 single float32 values, one to a partition and block"):
@@ -64,15 +60,15 @@ def tile_gather_matmul_kernel(tc, table, w, b, offs, out):
 
         banks = [psum.tile([P, V], F32, name="bank%d" % mb) for mb in range(M_BLOCKS)]
         order = [(0, 0), (0, 1), (1, 0), (1, 1), (LATE, 0), (2, 0), (2, 1), (LATE, 1)]
+        last_block = [2, LATE]
         for kb, mb in order:
-            ends = (0, 1) if kb == 0 else (1, 0)
-            for end in ends:
+            for end in range(ENDS):
                 nc.tensor.matmul(
                     banks[mb][:],
-                    weights_of[(kb, end, mb)],
+                    weights_of[(end, kb * M + mb * P)],
                     table_blocks[kb][:].indirect(offsets[:, end * LIST_COLUMNS : (end + 1) * LIST_COLUMNS]),
-                    start=(kb == 0 and end == ends[0]),
-                    stop=(kb == (LATE if mb == 1 else 2) and end == ends[1]),
+                    start=(kb == 0 and end == 0),
+                    stop=(kb == last_block[mb] and end == ENDS - 1),
                 )
 
         for mb in range(M_BLOCKS):

import concourse.mybir as mybir

BF16 = mybir.dt.bfloat16
F32 = mybir.dt.float32
U16 = mybir.dt.uint16
SILU = mybir.ActivationFunctionType.Silu

P = 128
K, S = 512, 2048
ENDS, M, V = 2, 256, 512
K_BLOCKS = K // P
M_BLOCKS = M // P
HALF = V // 2
LATE = K_BLOCKS - 1
LIST_COLUMNS = V // 16

FLOPS = 2 * ENDS * K * M * V


def tile_gather_matmul_kernel(tc, table, w, b, offs, out):
    nc = tc.nc
    with (
        tc.tile_pool(name="held", bufs=1) as held,
        tc.psum_pool(name="psum", bufs=1) as psum,
    ):
        offsets = held.tile([P, ENDS * LIST_COLUMNS], U16, name="offsets")
        nc.sync.dma_start(offsets[:], offs)

        table_dealt = table.rearrange("(p kb) s -> p kb s", kb=K_BLOCKS)
        w_dealt = w.rearrange("t (p kb) m -> p t (kb m)", kb=K_BLOCKS)
        table_blocks = [held.tile([P, S], BF16, name="table%d" % kb) for kb in range(K_BLOCKS)]
        weights_of = {}

        def load_weights(queue, ends, first, last):
            piece = held.tile([P, ends.stop - ends.start, last - first], BF16, name="weights%d_%d" % (ends.start, first))
            queue.dma_start(piece[:], w_dealt[:, ends, first:last])
            for end in range(ends.start, ends.stop):
                for column in range(first, last, P):
                    weights_of[(end, column)] = piece[:, end - ends.start, column - first : column - first + P]

        def load_table(kb):
            nc.scalar.dma_start(table_blocks[kb][:], table_dealt[:, kb, :])

        sources, targets, both = slice(0, 1), slice(1, 2), slice(0, 2)
        late_column = LATE * M + P
        load_weights(nc.sync, sources, 0, P)
        load_table(0)
        load_weights(nc.scalar, sources, P, M)
        load_weights(nc.scalar, targets, 0, M)
        load_table(1)
        load_weights(nc.scalar, sources, M, late_column)
        load_weights(nc.scalar, targets, M, late_column)
        load_table(LATE)
        load_table(2)
        load_weights(nc.scalar, both, late_column, late_column + P)

        bias = held.tile([P, M_BLOCKS], F32, name="bias")
        with nc.allow_non_contiguous_dma(reason="256 single float32 values, one to a partition and block"):
            nc.scalar.dma_start(bias[:], b.rearrange("(a p) o -> p (a o)", p=P))

        banks = [psum.tile([P, V], F32, name="bank%d" % mb) for mb in range(M_BLOCKS)]
        order = [(0, 0), (0, 1), (1, 0), (1, 1), (LATE, 0), (2, 0), (2, 1), (LATE, 1)]
        last_block = [2, LATE]
        for kb, mb in order:
            for end in range(ENDS):
                nc.tensor.matmul(
                    banks[mb][:],
                    weights_of[(end, kb * M + mb * P)],
                    table_blocks[kb][:].indirect(offsets[:, end * LIST_COLUMNS : (end + 1) * LIST_COLUMNS]),
                    start=(kb == 0 and end == 0),
                    stop=(kb == last_block[mb] and end == ENDS - 1),
                )

        for mb in range(M_BLOCKS):
            for half in range(2):
                columns = slice(half * HALF, (half + 1) * HALF)
                result = held.tile([P, HALF], F32, name="result%d_%d" % (mb, half))
                nc.scalar.activation(result[:], banks[mb][:, columns], SILU, bias=bias[:, mb : mb + 1])
                nc.sync.dma_start(out[mb * P : (mb + 1) * P, columns], result[:])
